import numpy as np
import ml_dtypes


def mxq(x, axis, fmt="e4m3"):
    dtype, down = {"e4m3": (ml_dtypes.float8_e4m3fn, 7), "e5m2": (ml_dtypes.float8_e5m2, 14)}[fmt]
    v = np.moveaxis(np.asarray(x, np.float32).astype(ml_dtypes.bfloat16).astype(np.float64), axis, -1)
    blocks = v.reshape(v.shape[:-1] + (-1, 32))
    amax = np.abs(blocks).max(-1, keepdims=True)
    byte = np.maximum(np.where(amax > 0, np.frexp(amax)[1] - 1 + 127, 0) - down, 1)
    scale = np.exp2(byte - 127.0)
    codes = (blocks / scale).astype(np.float32).astype(dtype).astype(np.float64)
    return np.moveaxis((codes * scale).reshape(v.shape), -1, axis)


WIDE = False


def mx_kscale(k):
    if not WIDE:
        return np.ones(k)
    levels = np.array([10, -10, 5, -5, 0])
    if k % 512:
        return np.exp2(np.random.permutation(np.resize(levels, k // 32))).repeat(32)
    a = np.empty((k // 512, 16))
    for p in range(k // 512):
        a[p, :8] = np.random.permutation(np.resize(levels, 8))
        for g in range(8):
            far = levels[np.abs(levels - a[p, g]) >= 10]
            a[p, g + 8] = far[np.random.randint(len(far))]
    return np.exp2(a.ravel()).repeat(32)


def f64(x):
    return np.asarray(x).astype(np.float64)


def striped(idx):
    return np.tile(idx.reshape(-1, 16).T, (8, 1)).astype(np.uint16)


def unstriped(offs):
    return offs[:16].T.reshape(-1).astype(np.int64)


def striped8(idx):
    return np.concatenate([x.reshape(-1, 16).T for x in idx]).astype(np.uint16)


def runs(offs, k):
    lists = np.stack([offs[16 * r : 16 * r + 16].T.reshape(-1) for r in range(8)]).astype(np.int64)
    return lists[np.arange(k) % 512 // 64]


def pack_weight(w):
    k, n = w.shape
    w = f64(np.asarray(w, np.float32).astype(ml_dtypes.bfloat16)).reshape(k // 32, 32, n)
    amax = np.abs(w).max(1)
    byte = np.clip(np.where(amax > 0, np.frexp(amax)[1] - 1 + 127 - 7, 1), 1, 254)
    scaled = (w * np.exp2(127.0 - byte)[:, None, :]).reshape(k, n).astype(np.float32)
    words = np.ascontiguousarray(scaled.reshape(k // 512, 128, 4, n).transpose(0, 1, 3, 2)).astype(ml_dtypes.float8_e4m3fn).view(np.uint8)
    return words, np.ascontiguousarray(byte.astype(np.uint8).reshape(k // 512, 16, n))


def unpack_weight(words, scales):
    g, p, n, _ = words.shape
    vals = np.ascontiguousarray(words).view(ml_dtypes.float8_e4m3fn).astype(np.float64) * np.repeat(np.exp2(scales.astype(np.float64) - 127.0), 8, axis=1)[..., None]
    return vals.transpose(0, 1, 3, 2).reshape(g * 512, n)


def sigmoid(v):
    return 1.0 / (1.0 + np.exp(-np.maximum(v, -700.0)))


K, T, S, N, G, H, W = 512, 1024, 256, 512, 2048, 512, 128


def setup_inputs():
    n = np.random.standard_normal
    s = mx_kscale(K)[:, None]
    u = mx_kscale(K)
    packed_xT = pack_weight(n((K, T)) * s)
    packed_dT = pack_weight(n((K, G)) / s)
    perm = np.random.permutation(S)
    return {
        "x_words": packed_xT[0],
        "x_scales": packed_xT[1],
        "d_words": packed_dT[0],
        "d_scales": packed_dT[1],
        "sl": np.random.uniform(1.0, 2.0, (H, 1)).astype(np.float32),
        "th": (0.5 * n((H, 1))).astype(np.float32),
        "tau": np.random.uniform(0.2, 0.6, (H, 1)).astype(np.float32),
        "tau2": np.random.uniform(0.6, 1.0, (H, 1)).astype(np.float32),
        "gn": (np.random.uniform(0.5, 1.5, (H, 1)) * u[:, None]).astype(np.float32),
        "gm": (np.random.uniform(0.5, 1.5, (H, 1)) * u[:, None]).astype(np.float32),
        "w1": (n((H, N)) / np.sqrt(2 * H) / u[:, None]).astype(np.float32),
        "w2": (n((H, N)) / np.sqrt(2 * H) / u[:, None]).astype(np.float32),
        "sl2": np.random.uniform(1.0, 2.0, (N, 1)).astype(np.float32),
        "th2": (0.5 * n((N, 1))).astype(np.float32),
        "offs": striped(np.random.permutation(T)[:S]),
        "k1": striped8(np.random.randint(0, G, (8, H))),
        "two": striped(np.random.permutation(T)[:S]),
        "k2": striped8(np.random.randint(0, G, (8, H))),
        "n1": striped(perm[:W]),
        "n2": striped(perm[W:]),
        "n3": striped(np.random.permutation(S)),
        "n4": striped(np.random.permutation(S)),
        "n5": striped(np.random.permutation(S)),
        "n6": striped(np.random.permutation(S)),
    }


def reference(x_words, x_scales, d_words, d_scales, sl, th, tau, tau2, gn, gm, w1, w2, sl2, th2, offs, k1, two, k2, n1, n2, n3, n4, n5, n6):
    d_k1 = unpack_weight(d_words, d_scales)[np.arange(K)[:, None], runs(k1, K)]
    xq = unpack_weight(x_words, x_scales)[:, unstriped(offs)]
    a = 0.0625 * (d_k1.T @ xq)
    pb = a[:, unstriped(n2)]
    sg = sigmoid(f64(sl) * (a[:, unstriped(n1)] - f64(th)))
    rb = pb - sg
    pa = a[:, unstriped(n1)]
    sg2 = sigmoid(f64(sl) * (a[:, unstriped(n2)] - f64(th)))
    ra = pa * sg2
    ds = np.zeros((H, S))
    ds[:, unstriped(n1)] = ra
    dt = ds.copy()
    dt[:, unstriped(n2)] = rb
    z = f64(gn) * dt
    d_k2 = unpack_weight(d_words, d_scales)[np.arange(K)[:, None], runs(k2, K)]
    x_two = unpack_weight(x_words, x_scales)[:, unstriped(two)]
    b = 0.0625 * (d_k2.T @ x_two)
    top = b.max(axis=1, keepdims=True)
    ea = np.exp(f64(tau) * (b[:, unstriped(n3)] - top))
    ea2 = np.exp(f64(tau2) * (b[:, unstriped(n4)] - top))
    z2 = f64(gm) * (3.0 * (ea - ea2))
    h = mxq(f64(w1), 0, "e4m3").T @ mxq(z, 0, "e4m3") + mxq(f64(w2), 0, "e4m3").T @ mxq(z2, 0, "e4m3")
    sg3 = sigmoid(f64(sl2) * (h[:, unstriped(n6)] - f64(th2)))
    return h + sg3 * (h[:, unstriped(n5)] - h)

@@ -1,0 +1,238 @@
+from contextlib import ExitStack
+
+import concourse.mybir as mybir
+
+K, T, S, N, G, H, W = 512, 1024, 256, 512, 2048, 512, 128
+FLOPS = 2 * 2 * K * H * S + 2 * 2 * H * N * S
+
+F32 = mybir.dt.float32
+BF16 = mybir.dt.bfloat16
+I32 = mybir.dt.int32
+U32 = mybir.dt.uint32
+U16 = mybir.dt.uint16
+U8 = mybir.dt.uint8
+FP8X4 = mybir.dt.float8_e4m3fn_x4
+ALU = mybir.AluOpType
+ACT = mybir.ActivationFunctionType
+
+P = 128
+PACK = 4
+
+
+def tile_picked_pqjeodetwetr_none_p_kernel(
+    tc, x_words, x_scales, d_words, d_scales, sl, th, tau, tau2, gn, gm, w1, w2, sl2, th2,
+    offs, k1, two, k2, n1, n2, n3, n4, n5, n6, out,
+):
+    nc = tc.nc
+    with ExitStack() as ctx:
+        lists = ctx.enter_context(tc.tile_pool(name="lists", bufs=1))
+        keep = ctx.enter_context(tc.tile_pool(name="keep", bufs=1))
+        psum = ctx.enter_context(tc.psum_pool(name="psum", bufs=1))
+
+        def sb(shape, dtype, name, tag=None):
+            return keep.tile(shape, dtype, name=name, tag=tag or name, align_bytes=64)
+
+        def load_list(src, name):
+            tile = lists.tile(list(src.shape), U16, name=name)
+            nc.sync.dma_start(tile[:], src)
+            return tile
+
+        def load_rows(src, name, pattern):
+            tile = sb([P, PACK], F32, name)
+            with nc.allow_non_contiguous_dma(reason="four values a partition"):
+                nc.gpsimd.dma_start(out=tile[:], in_=src.rearrange(pattern, t=PACK))
+            return tile
+
+        def minus_product(slope, threshold, name):
+            product = sb([P, PACK], F32, name + "_plus")
+            nc.gpsimd.tensor_tensor(product[:], slope[:], threshold[:], ALU.mult)
+            bias = sb([P, PACK], F32, name)
+            nc.gpsimd.tensor_scalar(bias[:], product[:], -1.0, 0.0, ALU.mult, ALU.add)
+            return bias
+
+        d_sc = sb([P, G], U8, "d_sc")
+        x_sc = sb([P, T], U8, "x_sc")
+        nc.vector.memset(d_sc[:].bitcast(I32), 0)
+        nc.vector.memset(x_sc[:].bitcast(I32), 0)
+        d_w = sb([P, G], U32, "d_w")
+        x_w = sb([P, T], U32, "x_w")
+
+        k1_t = load_list(k1, "k1_t")
+        nc.scalar.dma_start(out=d_w[:].bitcast(I32), in_=d_words[0].rearrange("p n r -> p (n r)").bitcast(I32))
+        nc.sync.dma_start(out=d_sc[:].bitcast(I32)[0:P:8, :], in_=d_scales[0].bitcast(I32))
+        nc.scalar.dma_start(out=x_w[:].bitcast(I32), in_=x_words[0].rearrange("p n r -> p (n r)").bitcast(I32))
+        nc.sync.dma_start(out=x_sc[:].bitcast(I32)[0:P:8, :], in_=x_scales[0].bitcast(I32))
+        offs_t = load_list(offs, "offs_t")
+        n1_t = load_list(n1, "n1_t")
+        n2_t = load_list(n2, "n2_t")
+        k2_t = load_list(k2, "k2_t")
+        two_t = load_list(two, "two_t")
+        n3_t = load_list(n3, "n3_t")
+        n4_t = load_list(n4, "n4_t")
+        n5_t = load_list(n5, "n5_t")
+        n6_t = load_list(n6, "n6_t")
+
+        dealt = "(p t) o -> p (t o)"
+        plain = "(t p) o -> p (t o)"
+        sl_t = load_rows(sl, "sl_t", dealt)
+        th_t = load_rows(th, "th_t", dealt)
+        gn_t = load_rows(gn, "gn_t", dealt)
+        tau_t = load_rows(tau, "tau_t", dealt)
+        tau2_t = load_rows(tau2, "tau2_t", dealt)
+        gm_t = load_rows(gm, "gm_t", dealt)
+        gm3 = sb([P, PACK], F32, "gm3")
+        nc.gpsimd.tensor_scalar(gm3[:], gm_t[:], 3.0, 0.0, ALU.mult, ALU.add)
+        sl2_t = load_rows(sl2, "sl2_t", plain)
+        th2_t = load_rows(th2, "th2_t", plain)
+        sig2_bias = minus_product(sl2_t, th2_t, "sig2_bias")
+
+        placed = [sb([P, H + S], U8, "placed_%d" % u) for u in range(2)]
+        for u in range(2):
+            nc.vector.memset(placed[u][:].bitcast(I32), 0)
+        wide = [sb([P, 2 * S], F32, "wide_%d" % t) for t in range(PACK)]
+        for t in range(PACK):
+            nc.vector.memset(wide[t][:, S:], 0.0)
+
+        def coded_product(u, codes, tokens, tags):
+            picked_sc = sb([P, H + S], U8, "picked_sc_%d" % u, tags[0])
+            nc.vector.tensor_copy(picked_sc[:, :H], d_sc[:].indirect(codes[:]))
+            nc.vector.tensor_copy(picked_sc[:, H:], x_sc[:].indirect(tokens[:]))
+            for s in range(4):
+                nc.scalar.dma_start(out=placed[u][:].bitcast(I32)[s:P:32, :],
+                                    in_=picked_sc[:].bitcast(I32)[8 * s:P:32, :])
+            picked_d = sb([P, H], U32, "picked_d_%d" % u, tags[1])
+            nc.vector.tensor_copy(picked_d[:], d_w[:].indirect(codes[:]))
+            dealt_d = sb([P, H], U32, "dealt_d_%d" % u, tags[2])
+            nc.vector.tensor_copy(dealt_d[:].rearrange("p (t m) -> p m t", t=PACK),
+                                  picked_d[:].rearrange("p (m t) -> p m t", t=PACK))
+            picked_x = sb([P, S], U32, "picked_x_%d" % u, tags[3])
+            nc.vector.tensor_copy(picked_x[:], x_w[:].indirect(tokens[:]))
+            dealt_sc = sb([P, H], U8, "dealt_sc_%d" % u, tags[4])
+            nc.vector.tensor_copy(dealt_sc[:].rearrange("p (t m) -> p m t", t=PACK),
+                                  placed[u][:, :H].rearrange("p (m t) -> p m t", t=PACK))
+            banks = []
+            for t in range(PACK):
+                bank = psum.tile([P, S], F32, name="acc_%d_%d" % (u, t), tag="bank_%d_%d" % (u, t))
+                cols = slice(t * P, (t + 1) * P)
+                nc.tensor.matmul_mx(out=bank[:], lhsT=dealt_d[:, cols].bitcast(FP8X4), lhsT_scale=dealt_sc[:, cols],
+                                    rhs=picked_x[:].bitcast(FP8X4), rhs_scale=placed[u][:, H:], start=True, stop=True)
+                banks.append(bank)
+            return banks
+
+        def quantize_weight(src, name, tag):
+            raw = sb([P, PACK, N], F32, name + "_raw", tag)
+            nc.sync.dma_start(out=raw[:], in_=src.rearrange("(p t) m -> p t m", t=PACK))
+            woven = sb([P, N, PACK], BF16, name + "_woven")
+            nc.vector.tensor_copy(woven[:].rearrange("p (c i) t -> p c t i", i=4),
+                                  raw[:].rearrange("p t (c i) -> p c t i", i=4))
+            codes = sb([P, N], U32, name + "_codes")
+            scales = sb([P, N], U8, name + "_scales")
+            nc.vector.quantize_mx(out=codes[:].bitcast(FP8X4), scales=scales[:],
+                                  in_=woven[:].rearrange("p c t -> p (c t)"))
+            return codes, scales
+
+        def quantize_planes(planes, name):
+            woven = sb([P, S, PACK], BF16, name + "_woven")
+            nc.vector.tensor_copy(woven[:].rearrange("p (c i) t -> p c t i", i=4),
+                                  planes[:].rearrange("p t (c i) -> p c t i", i=4))
+            codes = sb([P, S], U32, name + "_codes")
+            scales = sb([P, S], U8, name + "_scales")
+            nc.vector.quantize_mx(out=codes[:].bitcast(FP8X4), scales=scales[:],
+                                  in_=woven[:].rearrange("p c t -> p (c t)"))
+            return codes, scales
+
+        a_banks = coded_product(0, k1_t, offs_t, ["sc_a", "wd_a", "wd_b", "wx", "sc_b"])
+        sig_bias = sb([P, PACK], F32, "sig_bias")
+        nc.vector.scalar_tensor_tensor(sig_bias[:], sl_t[:], -1.0, th_t[:], ALU.mult, ALU.mult)
+        a_sb = []
+        for t in range(PACK):
+            a_t = sb([P, S], F32, "a_%d" % t)
+            nc.vector.tensor_scalar(a_t[:], a_banks[t][:], 0.0625, None, ALU.mult)
+            a_sb.append(a_t)
+        gates = sb([P, PACK, 2, W], F32, "gates", "gates")
+        pairs = sb([P, PACK, 2, W], F32, "pairs")
+        mixed = sb([P, PACK, 2, W], F32, "mixed")
+        for t in range(PACK):
+            col = slice(t, t + 1)
+            nc.scalar.activation(gates[:, t, 0, :], a_sb[t][:].indirect(n2_t[:]), ACT.Sigmoid,
+                                 bias=sig_bias[:, col], scale=sl_t[:, col])
+            nc.scalar.activation(pairs[:, t, 0, :], a_sb[t][:].indirect(n1_t[:]), ACT.Copy)
+            nc.scalar.activation(gates[:, t, 1, :], a_sb[t][:].indirect(n1_t[:]), ACT.Sigmoid,
+                                 bias=sig_bias[:, col], scale=sl_t[:, col])
+            nc.scalar.activation(pairs[:, t, 1, :], a_sb[t][:].indirect(n2_t[:]), ACT.Copy)
+            nc.vector.tensor_tensor(mixed[:, t, 0, :], pairs[:, t, 0, :], gates[:, t, 0, :], ALU.mult)
+            nc.vector.tensor_tensor(mixed[:, t, 1, :], pairs[:, t, 1, :], gates[:, t, 1, :], ALU.subtract)
+
+        b_banks = coded_product(1, k2_t, two_t, ["sc_b", "wd_b", "wd_a", "wx", "dealt_sc_1"])
+        top = sb([P, PACK], F32, "top")
+        for t in range(PACK):
+            nc.vector.tensor_scalar(wide[t][:, :S], b_banks[t][:], 0.0625, None, ALU.mult, ALU.max,
+                                    accum_out=top[:, t:t + 1])
+        exp_bias = sb([P, PACK], F32, "exp_bias")
+        exp_bias2 = sb([P, PACK], F32, "exp_bias2")
+        nc.vector.scalar_tensor_tensor(exp_bias[:], top[:], -1.0, tau_t[:], ALU.mult, ALU.mult)
+        nc.vector.scalar_tensor_tensor(exp_bias2[:], top[:], -1.0, tau2_t[:], ALU.mult, ALU.mult)
+
+        w1_codes, w1_scales = quantize_weight(w1, "w1", "sc_a")
+        w2_codes, w2_scales = quantize_weight(w2, "w2", "placed_0")
+        z_planes = sb([P, PACK, S], BF16, "z_planes", "w2_woven")
+        for t in range(PACK):
+            dt_t = sb([P, S], F32, "dt_%d" % t)
+            nc.scalar.activation(dt_t[:].indirect(n1_t[:]), mixed[:, t, 0, :], ACT.Copy)
+            nc.scalar.activation(dt_t[:].indirect(n2_t[:]), mixed[:, t, 1, :], ACT.Copy)
+            nc.vector.tensor_scalar(z_planes[:, t, :], dt_t[:], gn_t[:, t:t + 1], None, ALU.mult)
+
+        z_codes, z_scales = quantize_planes(z_planes, "z")
+        h_banks = []
+        for t in range(PACK):
+            bank = psum.tile([P, S], F32, name="h_acc_%d" % t, tag="bank_0_%d" % t)
+            cols = slice(t * P, (t + 1) * P)
+            nc.tensor.matmul_mx(out=bank[:], lhsT=w1_codes[:, cols].bitcast(FP8X4), lhsT_scale=w1_scales[:, cols],
+                                rhs=z_codes[:].bitcast(FP8X4), rhs_scale=z_scales[:], start=True, stop=False)
+            h_banks.append(bank)
+
+        ea2 = sb([P, PACK, S], F32, "ea2", "gates")
+        ea = sb([P, PACK, S], F32, "ea", "pairs")
+        ea2g = sb([P, PACK, S], F32, "ea2g")
+        z2_planes = sb([P, PACK, S], BF16, "z2_planes")
+        for t in range(PACK):
+            col = slice(t, t + 1)
+            nc.scalar.activation(ea2[:, t, :], wide[t][:].indirect(n4_t[:]), ACT.Exp,
+                                 bias=exp_bias2[:, col], scale=tau2_t[:, col])
+            nc.scalar.activation(ea[:, t, :], wide[t][:].indirect(n3_t[:]), ACT.Exp,
+                                 bias=exp_bias[:, col], scale=tau_t[:, col])
+            nc.vector.tensor_scalar(ea2g[:, t, :], ea2[:, t, :], gm3[:, col], None, ALU.mult)
+            nc.vector.scalar_tensor_tensor(z2_planes[:, t, :], ea[:, t, :], gm3[:, col], ea2g[:, t, :],
+                                           ALU.mult, ALU.subtract)
+        z2_codes, z2_scales = quantize_planes(z2_planes, "z2")
+        for t in range(PACK):
+            cols = slice(t * P, (t + 1) * P)
+            nc.tensor.matmul_mx(out=h_banks[t][:], lhsT=w2_codes[:, cols].bitcast(FP8X4), lhsT_scale=w2_scales[:, cols],
+                                rhs=z2_codes[:].bitcast(FP8X4), rhs_scale=z2_scales[:], start=False, stop=True)
+
+        for t in range(PACK):
+            col = slice(t, t + 1)
+            if t == 0:
+                nc.vector.tensor_copy(wide[t][:, :S], h_banks[t][:])
+            else:
+                nc.scalar.copy(wide[t][:, :S], h_banks[t][:])
+            gate = sb([P, S], F32, "gate_%d" % t)
+            res = sb([P, S], F32, "res_%d" % t)
+            far = sb([P, S], F32, "far_%d" % t)
+            near = sb([P, S], F32, "near_%d" % t)
+            if t == 0:
+                nc.vector.tensor_copy(far[:], wide[t][:].indirect(n5_t[:]))
+            if t == PACK - 1:
+                nc.scalar.activation(far[:], wide[t][:].indirect(n5_t[:]), ACT.Copy)
+            nc.scalar.activation(gate[:], wide[t][:].indirect(n6_t[:]), ACT.Sigmoid,
+                                 bias=sig2_bias[:, col], scale=sl2_t[:, col])
+            if t in (0, PACK - 1):
+                step = sb([P, S], F32, "step_%d" % t)
+                nc.vector.tensor_tensor(near[:], far[:], h_banks[t][:], ALU.subtract)
+                nc.vector.tensor_tensor(step[:], near[:], gate[:], ALU.mult)
+                nc.vector.tensor_tensor(res[:], step[:], h_banks[t][:], ALU.add)
+            else:
+                nc.vector.scalar_tensor_tensor(near[:], gate[:], 1.0, h_banks[t][:], ALU.subtract, ALU.mult)
+                nc.vector.tensor_tensor(far[:], wide[t][:].indirect(n5_t[:]), gate[:], ALU.mult)
+                nc.vector.tensor_tensor(res[:], far[:], near[:], ALU.subtract)
+            nc.sync.dma_start(out=out[t * P:(t + 1) * P, :], in_=res[:])

@@ -17,6 +17,7 @@ ACT = mybir.ActivationFunctionType
 
 P = 128
 PACK = 4
+FIRST = 512
 
 
 def tile_picked_pqjeodetwetr_none_p_kernel(
@@ -43,12 +44,10 @@ def tile_picked_pqjeodetwetr_none_p_kernel(
                 nc.gpsimd.dma_start(out=tile[:], in_=src.rearrange(pattern, t=PACK))
             return tile
 
-        def minus_product(slope, threshold, name):
-            product = sb([P, PACK], F32, name + "_plus")
-            nc.gpsimd.tensor_tensor(product[:], slope[:], threshold[:], ALU.mult)
-            bias = sb([P, PACK], F32, name)
-            nc.gpsimd.tensor_scalar(bias[:], product[:], -1.0, 0.0, ALU.mult, ALU.add)
-            return bias
+        def load_weight(src, lo, hi, name, tag):
+            raw = sb([P, PACK, hi - lo], F32, name, tag)
+            nc.sync.dma_start(out=raw[:], in_=src.rearrange("(p t) m -> p t m", t=PACK)[:, :, lo:hi])
+            return raw
 
         d_sc = sb([P, G], U8, "d_sc")
         x_sc = sb([P, T], U8, "x_sc")
@@ -57,20 +56,15 @@ def tile_picked_pqjeodetwetr_none_p_kernel(
         d_w = sb([P, G], U32, "d_w")
         x_w = sb([P, T], U32, "x_w")
 
+        d_flat = d_words[0].rearrange("p n r -> p (n r)").bitcast(I32)
         k1_t = load_list(k1, "k1_t")
-        nc.scalar.dma_start(out=d_w[:].bitcast(I32), in_=d_words[0].rearrange("p n r -> p (n r)").bitcast(I32))
+        nc.sync.dma_start(out=d_w[:].bitcast(I32)[:, :FIRST], in_=d_flat[:, :FIRST])
         nc.sync.dma_start(out=d_sc[:].bitcast(I32)[0:P:8, :], in_=d_scales[0].bitcast(I32))
-        nc.scalar.dma_start(out=x_w[:].bitcast(I32), in_=x_words[0].rearrange("p n r -> p (n r)").bitcast(I32))
         nc.sync.dma_start(out=x_sc[:].bitcast(I32)[0:P:8, :], in_=x_scales[0].bitcast(I32))
         offs_t = load_list(offs, "offs_t")
-        n1_t = load_list(n1, "n1_t")
-        n2_t = load_list(n2, "n2_t")
-        k2_t = load_list(k2, "k2_t")
-        two_t = load_list(two, "two_t")
-        n3_t = load_list(n3, "n3_t")
-        n4_t = load_list(n4, "n4_t")
-        n5_t = load_list(n5, "n5_t")
-        n6_t = load_list(n6, "n6_t")
+        nc.sync.dma_start(out=d_w[:].bitcast(I32)[:, FIRST:], in_=d_flat[:, FIRST:])
+        nc.sync.dma_start(out=x_w[:].bitcast(I32), in_=x_words[0].rearrange("p n r -> p (n r)").bitcast(I32))
+        w1_head = load_weight(w1, 0, P, "w1_head", "w1_head")
 
         dealt = "(p t) o -> p (t o)"
         plain = "(t p) o -> p (t o)"
@@ -84,7 +78,10 @@ def tile_picked_pqjeodetwetr_none_p_kernel(
         nc.gpsimd.tensor_scalar(gm3[:], gm_t[:], 3.0, 0.0, ALU.mult, ALU.add)
         sl2_t = load_rows(sl2, "sl2_t", plain)
         th2_t = load_rows(th2, "th2_t", plain)
-        sig2_bias = minus_product(sl2_t, th2_t, "sig2_bias")
+        sl2_th2 = sb([P, PACK], F32, "sl2_th2")
+        nc.gpsimd.tensor_tensor(sl2_th2[:], sl2_t[:], th2_t[:], ALU.mult)
+        sig2_bias = sb([P, PACK], F32, "sig2_bias")
+        nc.gpsimd.tensor_scalar(sig2_bias[:], sl2_th2[:], -1.0, 0.0, ALU.mult, ALU.add)
 
         placed = [sb([P, H + S], U8, "placed_%d" % u) for u in range(2)]
         for u in range(2):
@@ -98,7 +95,7 @@ def tile_picked_pqjeodetwetr_none_p_kernel(
             nc.vector.tensor_copy(picked_sc[:, :H], d_sc[:].indirect(codes[:]))
             nc.vector.tensor_copy(picked_sc[:, H:], x_sc[:].indirect(tokens[:]))
             for s in range(4):
-                nc.scalar.dma_start(out=placed[u][:].bitcast(I32)[s:P:32, :],
+                nc.sync.dma_start(out=placed[u][:].bitcast(I32)[s:P:32, :],
                                     in_=picked_sc[:].bitcast(I32)[8 * s:P:32, :])
             picked_d = sb([P, H], U32, "picked_d_%d" % u, tags[1])
             nc.vector.tensor_copy(picked_d[:], d_w[:].indirect(codes[:]))
@@ -119,30 +116,27 @@ def tile_picked_pqjeodetwetr_none_p_kernel(
                 banks.append(bank)
             return banks
 
-        def quantize_weight(src, name, tag):
-            raw = sb([P, PACK, N], F32, name + "_raw", tag)
-            nc.sync.dma_start(out=raw[:], in_=src.rearrange("(p t) m -> p t m", t=PACK))
-            woven = sb([P, N, PACK], BF16, name + "_woven")
-            nc.vector.tensor_copy(woven[:].rearrange("p (c i) t -> p c t i", i=4),
-                                  raw[:].rearrange("p t (c i) -> p c t i", i=4))
-            codes = sb([P, N], U32, name + "_codes")
-            scales = sb([P, N], U8, name + "_scales")
-            nc.vector.quantize_mx(out=codes[:].bitcast(FP8X4), scales=scales[:],
-                                  in_=woven[:].rearrange("p c t -> p (c t)"))
-            return codes, scales
-
-        def quantize_planes(planes, name):
-            woven = sb([P, S, PACK], BF16, name + "_woven")
+        def quantize_planes(planes, name, codes, scales):
+            width = planes.shape[2]
+            woven = sb([P, width, PACK], BF16, name + "_woven")
             nc.vector.tensor_copy(woven[:].rearrange("p (c i) t -> p c t i", i=4),
                                   planes[:].rearrange("p t (c i) -> p c t i", i=4))
-            codes = sb([P, S], U32, name + "_codes")
-            scales = sb([P, S], U8, name + "_scales")
-            nc.vector.quantize_mx(out=codes[:].bitcast(FP8X4), scales=scales[:],
+            nc.vector.quantize_mx(out=codes.bitcast(FP8X4), scales=scales,
                                   in_=woven[:].rearrange("p c t -> p (c t)"))
-            return codes, scales
+
+        def mx_tiles(width, name):
+            return sb([P, width], U32, name + "_codes"), sb([P, width], U8, name + "_scales")
 
         a_banks = coded_product(0, k1_t, offs_t, ["sc_a", "wd_a", "wd_b", "wx", "sc_b"])
-        sig_bias = sb([P, PACK], F32, "sig_bias")
+        n2_t = load_list(n2, "n2_t")
+        n1_t = load_list(n1, "n1_t")
+        k2_t = load_list(k2, "k2_t")
+        two_t = load_list(two, "two_t")
+        n4_t = load_list(n4, "n4_t")
+        n3_t = load_list(n3, "n3_t")
+        n5_t = load_list(n5, "n5_t")
+        n6_t = load_list(n6, "n6_t")
+        sig_bias = sb([P, PACK], F32, "sig_bias", "sc_a")
         nc.vector.scalar_tensor_tensor(sig_bias[:], sl_t[:], -1.0, th_t[:], ALU.mult, ALU.mult)
         a_sb = []
         for t in range(PACK):
@@ -163,7 +157,7 @@ def tile_picked_pqjeodetwetr_none_p_kernel(
             nc.vector.tensor_tensor(mixed[:, t, 0, :], pairs[:, t, 0, :], gates[:, t, 0, :], ALU.mult)
             nc.vector.tensor_tensor(mixed[:, t, 1, :], pairs[:, t, 1, :], gates[:, t, 1, :], ALU.subtract)
 
-        b_banks = coded_product(1, k2_t, two_t, ["sc_b", "wd_b", "wd_a", "wx", "dealt_sc_1"])
+        b_banks = coded_product(1, k2_t, two_t, ["sc_b", "wd_b", "dealt_d_1", "wx", "dealt_sc_1"])
         top = sb([P, PACK], F32, "top")
         for t in range(PACK):
             nc.vector.tensor_scalar(wide[t][:, :S], b_banks[t][:], 0.0625, None, ALU.mult, ALU.max,
@@ -173,8 +167,13 @@ def tile_picked_pqjeodetwetr_none_p_kernel(
         nc.vector.scalar_tensor_tensor(exp_bias[:], top[:], -1.0, tau_t[:], ALU.mult, ALU.mult)
         nc.vector.scalar_tensor_tensor(exp_bias2[:], top[:], -1.0, tau2_t[:], ALU.mult, ALU.mult)
 
-        w1_codes, w1_scales = quantize_weight(w1, "w1", "sc_a")
-        w2_codes, w2_scales = quantize_weight(w2, "w2", "placed_0")
+        w1_codes, w1_scales = mx_tiles(N, "w1")
+        w2_codes, w2_scales = mx_tiles(N, "w2")
+        w1_rest = load_weight(w1, P, N, "w1_rest", "wd_a")
+        w2_raw = load_weight(w2, 0, N, "w2_raw", "placed_0")
+        quantize_planes(w1_head, "w1_head", w1_codes[:, :P], w1_scales[:, :P])
+        quantize_planes(w1_rest, "w1_rest", w1_codes[:, P:], w1_scales[:, P:])
+        quantize_planes(w2_raw, "w2", w2_codes[:], w2_scales[:])
         z_planes = sb([P, PACK, S], BF16, "z_planes", "w2_woven")
         for t in range(PACK):
             dt_t = sb([P, S], F32, "dt_%d" % t)
@@ -182,7 +181,8 @@ def tile_picked_pqjeodetwetr_none_p_kernel(
             nc.scalar.activation(dt_t[:].indirect(n2_t[:]), mixed[:, t, 1, :], ACT.Copy)
             nc.vector.tensor_scalar(z_planes[:, t, :], dt_t[:], gn_t[:, t:t + 1], None, ALU.mult)
 
-        z_codes, z_scales = quantize_planes(z_planes, "z")
+        z_codes, z_scales = mx_tiles(S, "z")
+        quantize_planes(z_planes, "z", z_codes[:], z_scales[:])
         h_banks = []
         for t in range(PACK):
             bank = psum.tile([P, S], F32, name="h_acc_%d" % t, tag="bank_0_%d" % t)
@@ -204,35 +204,52 @@ def tile_picked_pqjeodetwetr_none_p_kernel(
             nc.vector.tensor_scalar(ea2g[:, t, :], ea2[:, t, :], gm3[:, col], None, ALU.mult)
             nc.vector.scalar_tensor_tensor(z2_planes[:, t, :], ea[:, t, :], gm3[:, col], ea2g[:, t, :],
                                            ALU.mult, ALU.subtract)
-        z2_codes, z2_scales = quantize_planes(z2_planes, "z2")
+        first_bias = wide[2][:, 0:1]
+        first_scale = wide[3][:, 0:1]
+        nc.vector.tensor_copy(first_bias, sig2_bias[:, 0:1])
+        nc.vector.tensor_copy(first_scale, sl2_t[:, 0:1])
+        z2_codes, z2_scales = mx_tiles(S, "z2")
+        quantize_planes(z2_planes, "z2", z2_codes[:], z2_scales[:])
         for t in range(PACK):
             cols = slice(t * P, (t + 1) * P)
             nc.tensor.matmul_mx(out=h_banks[t][:], lhsT=w2_codes[:, cols].bitcast(FP8X4), lhsT_scale=w2_scales[:, cols],
                                 rhs=z2_codes[:].bitcast(FP8X4), rhs_scale=z2_scales[:], start=False, stop=True)
 
-        for t in range(PACK):
-            col = slice(t, t + 1)
-            if t == 0:
-                nc.vector.tensor_copy(wide[t][:, :S], h_banks[t][:])
-            else:
-                nc.scalar.copy(wide[t][:, :S], h_banks[t][:])
-            gate = sb([P, S], F32, "gate_%d" % t)
-            res = sb([P, S], F32, "res_%d" % t)
-            far = sb([P, S], F32, "far_%d" % t)
-            near = sb([P, S], F32, "near_%d" % t)
-            if t == 0:
-                nc.vector.tensor_copy(far[:], wide[t][:].indirect(n5_t[:]))
-            if t == PACK - 1:
-                nc.scalar.activation(far[:], wide[t][:].indirect(n5_t[:]), ACT.Copy)
-            nc.scalar.activation(gate[:], wide[t][:].indirect(n6_t[:]), ACT.Sigmoid,
-                                 bias=sig2_bias[:, col], scale=sl2_t[:, col])
-            if t in (0, PACK - 1):
-                step = sb([P, S], F32, "step_%d" % t)
-                nc.vector.tensor_tensor(near[:], far[:], h_banks[t][:], ALU.subtract)
-                nc.vector.tensor_tensor(step[:], near[:], gate[:], ALU.mult)
-                nc.vector.tensor_tensor(res[:], step[:], h_banks[t][:], ALU.add)
-            else:
-                nc.vector.scalar_tensor_tensor(near[:], gate[:], 1.0, h_banks[t][:], ALU.subtract, ALU.mult)
-                nc.vector.tensor_tensor(far[:], wide[t][:].indirect(n5_t[:]), gate[:], ALU.mult)
-                nc.vector.tensor_tensor(res[:], far[:], near[:], ALU.subtract)
-            nc.sync.dma_start(out=out[t * P:(t + 1) * P, :], in_=res[:])
+        gate = [sb([P, S], F32, "gate_%d" % t) for t in range(PACK)]
+        far = [sb([P, S], F32, "far_%d" % t) for t in range(PACK)]
+        near = [sb([P, S], F32, "near_%d" % t) for t in range(PACK)]
+        res = [sb([P, S], F32, "res_%d" % t) for t in range(PACK)]
+
+        def gate_of(t):
+            bias, scale = (first_bias, first_scale) if t == 0 else (sig2_bias[:, t:t + 1], sl2_t[:, t:t + 1])
+            nc.scalar.activation(gate[t][:], wide[t][:].indirect(n6_t[:]), ACT.Sigmoid, bias=bias, scale=scale)
+
+        def mix_parts(t):
+            nc.vector.scalar_tensor_tensor(near[t][:], gate[t][:], 1.0, h_banks[t][:], ALU.subtract, ALU.mult)
+            nc.vector.tensor_tensor(far[t][:], wide[t][:].indirect(n5_t[:]), gate[t][:], ALU.mult)
+
+        def mix_and_store(t):
+            nc.vector.tensor_tensor(res[t][:], far[t][:], near[t][:], ALU.subtract)
+            nc.sync.dma_start(out=out[t * P:(t + 1) * P, :], in_=res[t][:])
+
+        nc.vector.tensor_copy(wide[0][:, :S], h_banks[0][:])
+        nc.vector.tensor_copy(wide[1][:, :S], h_banks[1][:])
+        gate_of(0)
+        gate_of(1)
+        nc.scalar.copy(wide[2][:, :S], h_banks[2][:])
+        nc.scalar.copy(wide[3][:, :S], h_banks[3][:])
+        gate_of(2)
+        last = PACK - 1
+        nc.scalar.activation(far[last][:], wide[last][:].indirect(n5_t[:]), ACT.Copy)
+        gate_of(last)
+        mix_parts(0)
+        mix_parts(1)
+        mix_and_store(0)
+        mix_parts(2)
+        mix_and_store(1)
+        step = sb([P, S], F32, "step")
+        nc.vector.tensor_tensor(near[last][:], far[last][:], h_banks[last][:], ALU.subtract)
+        mix_and_store(2)
+        nc.vector.tensor_tensor(step[:], near[last][:], gate[last][:], ALU.mult)
+        nc.vector.tensor_tensor(res[last][:], step[:], h_banks[last][:], ALU.add)
+        nc.sync.dma_start(out=out[last * P:, :], in_=res[last][:])

@@ -17,7 +17,7 @@ ACT = mybir.ActivationFunctionType
 
 P = 128
 PACK = 4
-FIRST = 512
+FIRST = 768
 
 
 def tile_picked_pqjeodetwetr_none_p_kernel(
@@ -44,10 +44,8 @@ def tile_picked_pqjeodetwetr_none_p_kernel(
                 nc.gpsimd.dma_start(out=tile[:], in_=src.rearrange(pattern, t=PACK))
             return tile
 
-        def load_weight(src, lo, hi, name, tag):
-            raw = sb([P, PACK, hi - lo], F32, name, tag)
-            nc.sync.dma_start(out=raw[:], in_=src.rearrange("(p t) m -> p t m", t=PACK)[:, :, lo:hi])
-            return raw
+        def load_weight(raw, src, lo, hi):
+            nc.sync.dma_start(out=raw[:, :, lo:hi], in_=src.rearrange("(p t) m -> p t m", t=PACK)[:, :, lo:hi])
 
         d_sc = sb([P, G], U8, "d_sc")
         x_sc = sb([P, T], U8, "x_sc")
@@ -62,9 +60,12 @@ def tile_picked_pqjeodetwetr_none_p_kernel(
         nc.sync.dma_start(out=d_sc[:].bitcast(I32)[0:P:8, :], in_=d_scales[0].bitcast(I32))
         nc.sync.dma_start(out=x_sc[:].bitcast(I32)[0:P:8, :], in_=x_scales[0].bitcast(I32))
         offs_t = load_list(offs, "offs_t")
+        n2_t = load_list(n2, "n2_t")
         nc.sync.dma_start(out=d_w[:].bitcast(I32)[:, FIRST:], in_=d_flat[:, FIRST:])
         nc.sync.dma_start(out=x_w[:].bitcast(I32), in_=x_words[0].rearrange("p n r -> p (n r)").bitcast(I32))
-        w1_head = load_weight(w1, 0, P, "w1_head", "w1_head")
+        w1_raw = sb([P, PACK, N], F32, "w1_raw")
+        w2_raw = sb([P, PACK, N], F32, "w2_raw")
+        load_weight(w1_raw, w1, 0, P)
 
         dealt = "(p t) o -> p (t o)"
         plain = "(t p) o -> p (t o)"
@@ -83,19 +84,17 @@ def tile_picked_pqjeodetwetr_none_p_kernel(
         sig2_bias = sb([P, PACK], F32, "sig2_bias")
         nc.gpsimd.tensor_scalar(sig2_bias[:], sl2_th2[:], -1.0, 0.0, ALU.mult, ALU.add)
 
-        placed = [sb([P, H + S], U8, "placed_%d" % u) for u in range(2)]
-        for u in range(2):
-            nc.vector.memset(placed[u][:].bitcast(I32), 0)
+        placed = sb([P, H + S], U8, "placed")
+        nc.vector.memset(placed[:].bitcast(I32), 0)
         wide = [sb([P, 2 * S], F32, "wide_%d" % t) for t in range(PACK)]
-        for t in range(PACK):
-            nc.vector.memset(wide[t][:, S:], 0.0)
 
-        def coded_product(u, codes, tokens, tags):
+        def coded_product(u, codes, tokens, tags, pieces):
             picked_sc = sb([P, H + S], U8, "picked_sc_%d" % u, tags[0])
             nc.vector.tensor_copy(picked_sc[:, :H], d_sc[:].indirect(codes[:]))
             nc.vector.tensor_copy(picked_sc[:, H:], x_sc[:].indirect(tokens[:]))
             for s in range(4):
-                nc.sync.dma_start(out=placed[u][:].bitcast(I32)[s:P:32, :],
+                queue = nc.scalar if u == 0 and s % 2 else nc.sync
+                queue.dma_start(out=placed[:].bitcast(I32)[s:P:32, :],
                                     in_=picked_sc[:].bitcast(I32)[8 * s:P:32, :])
             picked_d = sb([P, H], U32, "picked_d_%d" % u, tags[1])
             nc.vector.tensor_copy(picked_d[:], d_w[:].indirect(codes[:]))
@@ -105,14 +104,15 @@ def tile_picked_pqjeodetwetr_none_p_kernel(
             picked_x = sb([P, S], U32, "picked_x_%d" % u, tags[3])
             nc.vector.tensor_copy(picked_x[:], x_w[:].indirect(tokens[:]))
             dealt_sc = sb([P, H], U8, "dealt_sc_%d" % u, tags[4])
-            nc.vector.tensor_copy(dealt_sc[:].rearrange("p (t m) -> p m t", t=PACK),
-                                  placed[u][:, :H].rearrange("p (m t) -> p m t", t=PACK))
+            for lo, hi in pieces:
+                nc.vector.tensor_copy(dealt_sc[:].rearrange("p (t m) -> p m t", t=PACK)[:, :, lo:hi],
+                                      placed[:, :H].rearrange("p (m t) -> p m t", t=PACK)[:, :, lo:hi])
             banks = []
             for t in range(PACK):
                 bank = psum.tile([P, S], F32, name="acc_%d_%d" % (u, t), tag="bank_%d_%d" % (u, t))
                 cols = slice(t * P, (t + 1) * P)
                 nc.tensor.matmul_mx(out=bank[:], lhsT=dealt_d[:, cols].bitcast(FP8X4), lhsT_scale=dealt_sc[:, cols],
-                                    rhs=picked_x[:].bitcast(FP8X4), rhs_scale=placed[u][:, H:], start=True, stop=True)
+                                    rhs=picked_x[:].bitcast(FP8X4), rhs_scale=placed[:, H:], start=True, stop=True)
                 banks.append(bank)
             return banks
 
@@ -120,15 +120,14 @@ def tile_picked_pqjeodetwetr_none_p_kernel(
             width = planes.shape[2]
             woven = sb([P, width, PACK], BF16, name + "_woven")
             nc.vector.tensor_copy(woven[:].rearrange("p (c i) t -> p c t i", i=4),
-                                  planes[:].rearrange("p t (c i) -> p c t i", i=4))
+                                  planes.rearrange("p t (c i) -> p c t i", i=4))
             nc.vector.quantize_mx(out=codes.bitcast(FP8X4), scales=scales,
                                   in_=woven[:].rearrange("p c t -> p (c t)"))
 
         def mx_tiles(width, name):
             return sb([P, width], U32, name + "_codes"), sb([P, width], U8, name + "_scales")
 
-        a_banks = coded_product(0, k1_t, offs_t, ["sc_a", "wd_a", "wd_b", "wx", "sc_b"])
-        n2_t = load_list(n2, "n2_t")
+        a_banks = coded_product(0, k1_t, offs_t, ["sc_a", "wd_a", "wd_b", "wx", "sc_b"], [(0, 1), (1, PACK)])
         n1_t = load_list(n1, "n1_t")
         k2_t = load_list(k2, "k2_t")
         two_t = load_list(two, "two_t")
@@ -136,6 +135,8 @@ def tile_picked_pqjeodetwetr_none_p_kernel(
         n3_t = load_list(n3, "n3_t")
         n5_t = load_list(n5, "n5_t")
         n6_t = load_list(n6, "n6_t")
+        load_weight(w1_raw, w1, P, N)
+        load_weight(w2_raw, w2, 0, N)
         sig_bias = sb([P, PACK], F32, "sig_bias", "sc_a")
         nc.vector.scalar_tensor_tensor(sig_bias[:], sl_t[:], -1.0, th_t[:], ALU.mult, ALU.mult)
         a_sb = []
@@ -157,7 +158,7 @@ def tile_picked_pqjeodetwetr_none_p_kernel(
             nc.vector.tensor_tensor(mixed[:, t, 0, :], pairs[:, t, 0, :], gates[:, t, 0, :], ALU.mult)
             nc.vector.tensor_tensor(mixed[:, t, 1, :], pairs[:, t, 1, :], gates[:, t, 1, :], ALU.subtract)
 
-        b_banks = coded_product(1, k2_t, two_t, ["sc_b", "wd_b", "dealt_d_1", "wx", "dealt_sc_1"])
+        b_banks = coded_product(1, k2_t, two_t, ["sc_b", "wd_b", "w2_woven", "wx", "dealt_sc_1"], [(0, PACK)])
         top = sb([P, PACK], F32, "top")
         for t in range(PACK):
             nc.vector.tensor_scalar(wide[t][:, :S], b_banks[t][:], 0.0625, None, ALU.mult, ALU.max,
@@ -169,11 +170,8 @@ def tile_picked_pqjeodetwetr_none_p_kernel(
 
         w1_codes, w1_scales = mx_tiles(N, "w1")
         w2_codes, w2_scales = mx_tiles(N, "w2")
-        w1_rest = load_weight(w1, P, N, "w1_rest", "wd_a")
-        w2_raw = load_weight(w2, 0, N, "w2_raw", "placed_0")
-        quantize_planes(w1_head, "w1_head", w1_codes[:, :P], w1_scales[:, :P])
-        quantize_planes(w1_rest, "w1_rest", w1_codes[:, P:], w1_scales[:, P:])
-        quantize_planes(w2_raw, "w2", w2_codes[:], w2_scales[:])
+        quantize_planes(w1_raw[:], "w1", w1_codes[:], w1_scales[:])
+        quantize_planes(w2_raw[:], "w2", w2_codes[:], w2_scales[:])
         z_planes = sb([P, PACK, S], BF16, "z_planes", "w2_woven")
         for t in range(PACK):
             dt_t = sb([P, S], F32, "dt_%d" % t)
@@ -182,7 +180,7 @@ def tile_picked_pqjeodetwetr_none_p_kernel(
             nc.vector.tensor_scalar(z_planes[:, t, :], dt_t[:], gn_t[:, t:t + 1], None, ALU.mult)
 
         z_codes, z_scales = mx_tiles(S, "z")
-        quantize_planes(z_planes, "z", z_codes[:], z_scales[:])
+        quantize_planes(z_planes[:], "z", z_codes[:], z_scales[:])
         h_banks = []
         for t in range(PACK):
             bank = psum.tile([P, S], F32, name="h_acc_%d" % t, tag="bank_0_%d" % t)
@@ -191,25 +189,28 @@ def tile_picked_pqjeodetwetr_none_p_kernel(
                                 rhs=z_codes[:].bitcast(FP8X4), rhs_scale=z_scales[:], start=True, stop=False)
             h_banks.append(bank)
 
+        halves = [(0, S // 2), (S // 2, S)]
         ea2 = sb([P, PACK, S], F32, "ea2", "gates")
         ea = sb([P, PACK, S], F32, "ea", "pairs")
-        ea2g = sb([P, PACK, S], F32, "ea2g")
+        ea2g = sb([P, PACK, S], F32, "ea2g", "z_woven")
         z2_planes = sb([P, PACK, S], BF16, "z2_planes")
         for t in range(PACK):
             col = slice(t, t + 1)
             nc.scalar.activation(ea2[:, t, :], wide[t][:].indirect(n4_t[:]), ACT.Exp,
                                  bias=exp_bias2[:, col], scale=tau2_t[:, col])
-            nc.scalar.activation(ea[:, t, :], wide[t][:].indirect(n3_t[:]), ACT.Exp,
-                                 bias=exp_bias[:, col], scale=tau_t[:, col])
             nc.vector.tensor_scalar(ea2g[:, t, :], ea2[:, t, :], gm3[:, col], None, ALU.mult)
-            nc.vector.scalar_tensor_tensor(z2_planes[:, t, :], ea[:, t, :], gm3[:, col], ea2g[:, t, :],
-                                           ALU.mult, ALU.subtract)
+            for lo, hi in (halves if t == PACK - 1 else [(0, S)]):
+                nc.scalar.activation(ea[:, t, lo:hi], wide[t][:].indirect(n3_t[:, lo // 16:hi // 16]), ACT.Exp,
+                                     bias=exp_bias[:, col], scale=tau_t[:, col])
+                nc.vector.scalar_tensor_tensor(z2_planes[:, t, lo:hi], ea[:, t, lo:hi], gm3[:, col],
+                                               ea2g[:, t, lo:hi], ALU.mult, ALU.subtract)
         first_bias = wide[2][:, 0:1]
         first_scale = wide[3][:, 0:1]
         nc.vector.tensor_copy(first_bias, sig2_bias[:, 0:1])
         nc.vector.tensor_copy(first_scale, sl2_t[:, 0:1])
         z2_codes, z2_scales = mx_tiles(S, "z2")
-        quantize_planes(z2_planes, "z2", z2_codes[:], z2_scales[:])
+        for lo, hi in halves:
+            quantize_planes(z2_planes[:, :, lo:hi], "z2_%d" % lo, z2_codes[:, lo:hi], z2_scales[:, lo:hi])
         for t in range(PACK):
             cols = slice(t * P, (t + 1) * P)
             nc.tensor.matmul_mx(out=h_banks[t][:], lhsT=w2_codes[:, cols].bitcast(FP8X4), lhsT_scale=w2_scales[:, cols],
@@ -242,14 +243,19 @@ def tile_picked_pqjeodetwetr_none_p_kernel(
         last = PACK - 1
         nc.scalar.activation(far[last][:], wide[last][:].indirect(n5_t[:]), ACT.Copy)
         gate_of(last)
-        mix_parts(0)
+        step = [sb([P, S], F32, "step_%d" % t) for t in range(2)]
+        nc.vector.tensor_copy(far[0][:], wide[0][:].indirect(n5_t[:]))
+        nc.vector.tensor_tensor(near[0][:], far[0][:], h_banks[0][:], ALU.subtract)
         mix_parts(1)
-        mix_and_store(0)
-        mix_parts(2)
+        nc.vector.tensor_tensor(step[0][:], near[0][:], gate[0][:], ALU.mult)
+        nc.vector.tensor_tensor(res[0][:], step[0][:], h_banks[0][:], ALU.add)
+        nc.sync.dma_start(out=out[:P, :], in_=res[0][:])
         mix_and_store(1)
-        step = sb([P, S], F32, "step")
+        mix_parts(2)
         nc.vector.tensor_tensor(near[last][:], far[last][:], h_banks[last][:], ALU.subtract)
         mix_and_store(2)
-        nc.vector.tensor_tensor(step[:], near[last][:], gate[last][:], ALU.mult)
-        nc.vector.tensor_tensor(res[last][:], step[:], h_banks[last][:], ALU.add)
-        nc.sync.dma_start(out=out[last * P:, :], in_=res[last][:])
+        for lo, hi in halves:
+            nc.vector.tensor_tensor(step[1][:, lo:hi], near[last][:, lo:hi], gate[last][:, lo:hi], ALU.mult)
+        for lo, hi in halves:
+            nc.vector.tensor_tensor(res[last][:, lo:hi], step[1][:, lo:hi], h_banks[last][:, lo:hi], ALU.add)
+            nc.sync.dma_start(out=out[last * P:, lo:hi], in_=res[last][:, lo:hi])

@@ -17,7 +17,7 @@ ACT = mybir.ActivationFunctionType
 
 P = 128
 PACK = 4
-FIRST = 768
+FIRST = 512
 
 
 def tile_picked_pqjeodetwetr_none_p_kernel(
@@ -38,10 +38,10 @@ def tile_picked_pqjeodetwetr_none_p_kernel(
             nc.sync.dma_start(tile[:], src)
             return tile
 
-        def load_rows(src, name, pattern):
+        def load_rows(queue, src, name, pattern):
             tile = sb([P, PACK], F32, name)
             with nc.allow_non_contiguous_dma(reason="four values a partition"):
-                nc.gpsimd.dma_start(out=tile[:], in_=src.rearrange(pattern, t=PACK))
+                queue.dma_start(out=tile[:], in_=src.rearrange(pattern, t=PACK))
             return tile
 
         def load_weight(raw, src, lo, hi):
@@ -55,34 +55,21 @@ def tile_picked_pqjeodetwetr_none_p_kernel(
         x_w = sb([P, T], U32, "x_w")
 
         d_flat = d_words[0].rearrange("p n r -> p (n r)").bitcast(I32)
+        dealt = "(p t) o -> p (t o)"
+        plain = "(t p) o -> p (t o)"
         k1_t = load_list(k1, "k1_t")
+        sl_t = load_rows(nc.scalar, sl, "sl_t", dealt)
+        th_t = load_rows(nc.scalar, th, "th_t", dealt)
         nc.sync.dma_start(out=d_w[:].bitcast(I32)[:, :FIRST], in_=d_flat[:, :FIRST])
         nc.sync.dma_start(out=d_sc[:].bitcast(I32)[0:P:8, :], in_=d_scales[0].bitcast(I32))
         nc.sync.dma_start(out=x_sc[:].bitcast(I32)[0:P:8, :], in_=x_scales[0].bitcast(I32))
         offs_t = load_list(offs, "offs_t")
-        n2_t = load_list(n2, "n2_t")
         nc.sync.dma_start(out=d_w[:].bitcast(I32)[:, FIRST:], in_=d_flat[:, FIRST:])
         nc.sync.dma_start(out=x_w[:].bitcast(I32), in_=x_words[0].rearrange("p n r -> p (n r)").bitcast(I32))
+        n2_t = load_list(n2, "n2_t")
         w1_raw = sb([P, PACK, N], F32, "w1_raw")
         w2_raw = sb([P, PACK, N], F32, "w2_raw")
         load_weight(w1_raw, w1, 0, P)
-
-        dealt = "(p t) o -> p (t o)"
-        plain = "(t p) o -> p (t o)"
-        sl_t = load_rows(sl, "sl_t", dealt)
-        th_t = load_rows(th, "th_t", dealt)
-        gn_t = load_rows(gn, "gn_t", dealt)
-        tau_t = load_rows(tau, "tau_t", dealt)
-        tau2_t = load_rows(tau2, "tau2_t", dealt)
-        gm_t = load_rows(gm, "gm_t", dealt)
-        gm3 = sb([P, PACK], F32, "gm3")
-        nc.gpsimd.tensor_scalar(gm3[:], gm_t[:], 3.0, 0.0, ALU.mult, ALU.add)
-        sl2_t = load_rows(sl2, "sl2_t", plain)
-        th2_t = load_rows(th2, "th2_t", plain)
-        sl2_th2 = sb([P, PACK], F32, "sl2_th2")
-        nc.gpsimd.tensor_tensor(sl2_th2[:], sl2_t[:], th2_t[:], ALU.mult)
-        sig2_bias = sb([P, PACK], F32, "sig2_bias")
-        nc.gpsimd.tensor_scalar(sig2_bias[:], sl2_th2[:], -1.0, 0.0, ALU.mult, ALU.add)
 
         placed = sb([P, H + S], U8, "placed")
         nc.vector.memset(placed[:].bitcast(I32), 0)
@@ -137,6 +124,19 @@ def tile_picked_pqjeodetwetr_none_p_kernel(
         n6_t = load_list(n6, "n6_t")
         load_weight(w1_raw, w1, P, N)
         load_weight(w2_raw, w2, 0, N)
+        gn_t = load_rows(nc.sync, gn, "gn_t", dealt)
+        tau_t = load_rows(nc.sync, tau, "tau_t", dealt)
+        tau2_t = load_rows(nc.sync, tau2, "tau2_t", dealt)
+        gm_t = load_rows(nc.sync, gm, "gm_t", dealt)
+        gm3 = sb([P, PACK], F32, "gm3")
+        nc.gpsimd.tensor_scalar(gm3[:], gm_t[:], 3.0, 0.0, ALU.mult, ALU.add)
+        sl2_t = load_rows(nc.sync, sl2, "sl2_t", plain)
+        th2_t = load_rows(nc.sync, th2, "th2_t", plain)
+        sl2_th2 = sb([P, PACK], F32, "sl2_th2")
+        nc.gpsimd.tensor_tensor(sl2_th2[:], sl2_t[:], th2_t[:], ALU.mult)
+        sig2_bias = sb([P, PACK], F32, "sig2_bias")
+        nc.gpsimd.tensor_scalar(sig2_bias[:], sl2_th2[:], -1.0, 0.0, ALU.mult, ALU.add)
+
         sig_bias = sb([P, PACK], F32, "sig_bias", "sc_a")
         nc.vector.scalar_tensor_tensor(sig_bias[:], sl_t[:], -1.0, th_t[:], ALU.mult, ALU.mult)
         a_sb = []

from contextlib import ExitStack

import concourse.mybir as mybir

K, T, S, N, G, H, W = 512, 1024, 256, 512, 2048, 512, 128
FLOPS = 2 * 2 * K * H * S + 2 * 2 * H * N * S

F32 = mybir.dt.float32
BF16 = mybir.dt.bfloat16
I32 = mybir.dt.int32
U32 = mybir.dt.uint32
U16 = mybir.dt.uint16
U8 = mybir.dt.uint8
FP8X4 = mybir.dt.float8_e4m3fn_x4
ALU = mybir.AluOpType
ACT = mybir.ActivationFunctionType

P = 128
PACK = 4
FIRST = 512


def tile_picked_pqjeodetwetr_none_p_kernel(
    tc, x_words, x_scales, d_words, d_scales, sl, th, tau, tau2, gn, gm, w1, w2, sl2, th2,
    offs, k1, two, k2, n1, n2, n3, n4, n5, n6, out,
):
    nc = tc.nc
    with ExitStack() as ctx:
        lists = ctx.enter_context(tc.tile_pool(name="lists", bufs=1))
        keep = ctx.enter_context(tc.tile_pool(name="keep", bufs=1))
        psum = ctx.enter_context(tc.psum_pool(name="psum", bufs=1))

        def sb(shape, dtype, name, tag=None):
            return keep.tile(shape, dtype, name=name, tag=tag or name, align_bytes=64)

        def load_list(src, name):
            tile = lists.tile(list(src.shape), U16, name=name)
            nc.sync.dma_start(tile[:], src)
            return tile

        def load_rows(queue, src, name, pattern):
            tile = sb([P, PACK], F32, name)
            with nc.allow_non_contiguous_dma(reason="four values a partition"):
                queue.dma_start(out=tile[:], in_=src.rearrange(pattern, t=PACK))
            return tile

        def load_weight(raw, src, lo, hi):
            nc.sync.dma_start(out=raw[:, :, lo:hi], in_=src.rearrange("(p t) m -> p t m", t=PACK)[:, :, lo:hi])

        d_sc = sb([P, G], U8, "d_sc")
        x_sc = sb([P, T], U8, "x_sc")
        nc.vector.memset(d_sc[:].bitcast(I32), 0)
        nc.vector.memset(x_sc[:].bitcast(I32), 0)
        d_w = sb([P, G], U32, "d_w")
        x_w = sb([P, T], U32, "x_w")

        d_flat = d_words[0].rearrange("p n r -> p (n r)").bitcast(I32)
        dealt = "(p t) o -> p (t o)"
        plain = "(t p) o -> p (t o)"
        k1_t = load_list(k1, "k1_t")
        sl_t = load_rows(nc.scalar, sl, "sl_t", dealt)
        th_t = load_rows(nc.scalar, th, "th_t", dealt)
        nc.sync.dma_start(out=d_w[:].bitcast(I32)[:, :FIRST], in_=d_flat[:, :FIRST])
        nc.sync.dma_start(out=d_sc[:].bitcast(I32)[0:P:8, :], in_=d_scales[0].bitcast(I32))
        nc.sync.dma_start(out=x_sc[:].bitcast(I32)[0:P:8, :], in_=x_scales[0].bitcast(I32))
        offs_t = load_list(offs, "offs_t")
        nc.sync.dma_start(out=d_w[:].bitcast(I32)[:, FIRST:], in_=d_flat[:, FIRST:])
        nc.sync.dma_start(out=x_w[:].bitcast(I32), in_=x_words[0].rearrange("p n r -> p (n r)").bitcast(I32))
        n2_t = load_list(n2, "n2_t")
        w1_raw = sb([P, PACK, N], F32, "w1_raw")
        w2_raw = sb([P, PACK, N], F32, "w2_raw")
        load_weight(w1_raw, w1, 0, P)

        placed = sb([P, H + S], U8, "placed")
        nc.vector.memset(placed[:].bitcast(I32), 0)
        wide = [sb([P, 2 * S], F32, "wide_%d" % t) for t in range(PACK)]

        def coded_product(u, codes, tokens, tags, pieces):
            picked_sc = sb([P, H + S], U8, "picked_sc_%d" % u, tags[0])
            nc.vector.tensor_copy(picked_sc[:, :H], d_sc[:].indirect(codes[:]))
            nc.vector.tensor_copy(picked_sc[:, H:], x_sc[:].indirect(tokens[:]))
            for s in range(4):
                queue = nc.scalar if u == 0 and s % 2 else nc.sync
                queue.dma_start(out=placed[:].bitcast(I32)[s:P:32, :],
                                    in_=picked_sc[:].bitcast(I32)[8 * s:P:32, :])
            picked_d = sb([P, H], U32, "picked_d_%d" % u, tags[1])
            nc.vector.tensor_copy(picked_d[:], d_w[:].indirect(codes[:]))
            dealt_d = sb([P, H], U32, "dealt_d_%d" % u, tags[2])
            nc.vector.tensor_copy(dealt_d[:].rearrange("p (t m) -> p m t", t=PACK),
                                  picked_d[:].rearrange("p (m t) -> p m t", t=PACK))
            picked_x = sb([P, S], U32, "picked_x_%d" % u, tags[3])
            nc.vector.tensor_copy(picked_x[:], x_w[:].indirect(tokens[:]))
            dealt_sc = sb([P, H], U8, "dealt_sc_%d" % u, tags[4])
            for lo, hi in pieces:
                nc.vector.tensor_copy(dealt_sc[:].rearrange("p (t m) -> p m t", t=PACK)[:, :, lo:hi],
                                      placed[:, :H].rearrange("p (m t) -> p m t", t=PACK)[:, :, lo:hi])
            banks = []
            for t in range(PACK):
                bank = psum.tile([P, S], F32, name="acc_%d_%d" % (u, t), tag="bank_%d_%d" % (u, t))
                cols = slice(t * P, (t + 1) * P)
                nc.tensor.matmul_mx(out=bank[:], lhsT=dealt_d[:, cols].bitcast(FP8X4), lhsT_scale=dealt_sc[:, cols],
                                    rhs=picked_x[:].bitcast(FP8X4), rhs_scale=placed[:, H:], start=True, stop=True)
                banks.append(bank)
            return banks

        def quantize_planes(planes, name, codes, scales):
            width = planes.shape[2]
            woven = sb([P, width, PACK], BF16, name + "_woven")
            nc.vector.tensor_copy(woven[:].rearrange("p (c i) t -> p c t i", i=4),
                                  planes.rearrange("p t (c i) -> p c t i", i=4))
            nc.vector.quantize_mx(out=codes.bitcast(FP8X4), scales=scales,
                                  in_=woven[:].rearrange("p c t -> p (c t)"))

        def mx_tiles(width, name):
            return sb([P, width], U32, name + "_codes"), sb([P, width], U8, name + "_scales")

        a_banks = coded_product(0, k1_t, offs_t, ["sc_a", "wd_a", "wd_b", "wx", "sc_b"], [(0, 1), (1, PACK)])
        n1_t = load_list(n1, "n1_t")
        k2_t = load_list(k2, "k2_t")
        two_t = load_list(two, "two_t")
        n4_t = load_list(n4, "n4_t")
        n3_t = load_list(n3, "n3_t")
        n5_t = load_list(n5, "n5_t")
        n6_t = load_list(n6, "n6_t")
        load_weight(w1_raw, w1, P, N)
        load_weight(w2_raw, w2, 0, N)
        gn_t = load_rows(nc.sync, gn, "gn_t", dealt)
        tau_t = load_rows(nc.sync, tau, "tau_t", dealt)
        tau2_t = load_rows(nc.sync, tau2, "tau2_t", dealt)
        gm_t = load_rows(nc.sync, gm, "gm_t", dealt)
        gm3 = sb([P, PACK], F32, "gm3")
        nc.gpsimd.tensor_scalar(gm3[:], gm_t[:], 3.0, 0.0, ALU.mult, ALU.add)
        sl2_t = load_rows(nc.sync, sl2, "sl2_t", plain)
        th2_t = load_rows(nc.sync, th2, "th2_t", plain)
        sl2_th2 = sb([P, PACK], F32, "sl2_th2")
        nc.gpsimd.tensor_tensor(sl2_th2[:], sl2_t[:], th2_t[:], ALU.mult)
        sig2_bias = sb([P, PACK], F32, "sig2_bias")
        nc.gpsimd.tensor_scalar(sig2_bias[:], sl2_th2[:], -1.0, 0.0, ALU.mult, ALU.add)

        sig_bias = sb([P, PACK], F32, "sig_bias", "sc_a")
        nc.vector.scalar_tensor_tensor(sig_bias[:], sl_t[:], -1.0, th_t[:], ALU.mult, ALU.mult)
        a_sb = []
        for t in range(PACK):
            a_t = sb([P, S], F32, "a_%d" % t)
            nc.vector.tensor_scalar(a_t[:], a_banks[t][:], 0.0625, None, ALU.mult)
            a_sb.append(a_t)
        gates = sb([P, PACK, 2, W], F32, "gates", "gates")
        pairs = sb([P, PACK, 2, W], F32, "pairs")
        mixed = sb([P, PACK, 2, W], F32, "mixed")
        for t in range(PACK):
            col = slice(t, t + 1)
            nc.scalar.activation(gates[:, t, 0, :], a_sb[t][:].indirect(n2_t[:]), ACT.Sigmoid,
                                 bias=sig_bias[:, col], scale=sl_t[:, col])
            nc.scalar.activation(pairs[:, t, 0, :], a_sb[t][:].indirect(n1_t[:]), ACT.Copy)
            nc.scalar.activation(gates[:, t, 1, :], a_sb[t][:].indirect(n1_t[:]), ACT.Sigmoid,
                                 bias=sig_bias[:, col], scale=sl_t[:, col])
            nc.scalar.activation(pairs[:, t, 1, :], a_sb[t][:].indirect(n2_t[:]), ACT.Copy)
            nc.vector.tensor_tensor(mixed[:, t, 0, :], pairs[:, t, 0, :], gates[:, t, 0, :], ALU.mult)
            nc.vector.tensor_tensor(mixed[:, t, 1, :], pairs[:, t, 1, :], gates[:, t, 1, :], ALU.subtract)

        b_banks = coded_product(1, k2_t, two_t, ["sc_b", "wd_b", "w2_woven", "wx", "dealt_sc_1"], [(0, PACK)])
        top = sb([P, PACK], F32, "top")
        for t in range(PACK):
            nc.vector.tensor_scalar(wide[t][:, :S], b_banks[t][:], 0.0625, None, ALU.mult, ALU.max,
                                    accum_out=top[:, t:t + 1])
        exp_bias = sb([P, PACK], F32, "exp_bias")
        exp_bias2 = sb([P, PACK], F32, "exp_bias2")
        nc.vector.scalar_tensor_tensor(exp_bias[:], top[:], -1.0, tau_t[:], ALU.mult, ALU.mult)
        nc.vector.scalar_tensor_tensor(exp_bias2[:], top[:], -1.0, tau2_t[:], ALU.mult, ALU.mult)

        w1_codes, w1_scales = mx_tiles(N, "w1")
        w2_codes, w2_scales = mx_tiles(N, "w2")
        quantize_planes(w1_raw[:], "w1", w1_codes[:], w1_scales[:])
        quantize_planes(w2_raw[:], "w2", w2_codes[:], w2_scales[:])
        z_planes = sb([P, PACK, S], BF16, "z_planes", "w2_woven")
        for t in range(PACK):
            dt_t = sb([P, S], F32, "dt_%d" % t)
            nc.scalar.activation(dt_t[:].indirect(n1_t[:]), mixed[:, t, 0, :], ACT.Copy)
            nc.scalar.activation(dt_t[:].indirect(n2_t[:]), mixed[:, t, 1, :], ACT.Copy)
            nc.vector.tensor_scalar(z_planes[:, t, :], dt_t[:], gn_t[:, t:t + 1], None, ALU.mult)

        z_codes, z_scales = mx_tiles(S, "z")
        quantize_planes(z_planes[:], "z", z_codes[:], z_scales[:])
        h_banks = []
        for t in range(PACK):
            bank = psum.tile([P, S], F32, name="h_acc_%d" % t, tag="bank_0_%d" % t)
            cols = slice(t * P, (t + 1) * P)
            nc.tensor.matmul_mx(out=bank[:], lhsT=w1_codes[:, cols].bitcast(FP8X4), lhsT_scale=w1_scales[:, cols],
                                rhs=z_codes[:].bitcast(FP8X4), rhs_scale=z_scales[:], start=True, stop=False)
            h_banks.append(bank)

        halves = [(0, S // 2), (S // 2, S)]
        ea2 = sb([P, PACK, S], F32, "ea2", "gates")
        ea = sb([P, PACK, S], F32, "ea", "pairs")
        ea2g = sb([P, PACK, S], F32, "ea2g", "z_woven")
        z2_planes = sb([P, PACK, S], BF16, "z2_planes")
        for t in range(PACK):
            col = slice(t, t + 1)
            nc.scalar.activation(ea2[:, t, :], wide[t][:].indirect(n4_t[:]), ACT.Exp,
                                 bias=exp_bias2[:, col], scale=tau2_t[:, col])
            nc.vector.tensor_scalar(ea2g[:, t, :], ea2[:, t, :], gm3[:, col], None, ALU.mult)
            for lo, hi in (halves if t == PACK - 1 else [(0, S)]):
                nc.scalar.activation(ea[:, t, lo:hi], wide[t][:].indirect(n3_t[:, lo // 16:hi // 16]), ACT.Exp,
                                     bias=exp_bias[:, col], scale=tau_t[:, col])
                nc.vector.scalar_tensor_tensor(z2_planes[:, t, lo:hi], ea[:, t, lo:hi], gm3[:, col],
                                               ea2g[:, t, lo:hi], ALU.mult, ALU.subtract)
        first_bias = wide[2][:, 0:1]
        first_scale = wide[3][:, 0:1]
        nc.vector.tensor_copy(first_bias, sig2_bias[:, 0:1])
        nc.vector.tensor_copy(first_scale, sl2_t[:, 0:1])
        z2_codes, z2_scales = mx_tiles(S, "z2")
        for lo, hi in halves:
            quantize_planes(z2_planes[:, :, lo:hi], "z2_%d" % lo, z2_codes[:, lo:hi], z2_scales[:, lo:hi])
        for t in range(PACK):
            cols = slice(t * P, (t + 1) * P)
            nc.tensor.matmul_mx(out=h_banks[t][:], lhsT=w2_codes[:, cols].bitcast(FP8X4), lhsT_scale=w2_scales[:, cols],
                                rhs=z2_codes[:].bitcast(FP8X4), rhs_scale=z2_scales[:], start=False, stop=True)

        gate = [sb([P, S], F32, "gate_%d" % t) for t in range(PACK)]
        far = [sb([P, S], F32, "far_%d" % t) for t in range(PACK)]
        near = [sb([P, S], F32, "near_%d" % t) for t in range(PACK)]
        res = [sb([P, S], F32, "res_%d" % t) for t in range(PACK)]

        def gate_of(t):
            bias, scale = (first_bias, first_scale) if t == 0 else (sig2_bias[:, t:t + 1], sl2_t[:, t:t + 1])
            nc.scalar.activation(gate[t][:], wide[t][:].indirect(n6_t[:]), ACT.Sigmoid, bias=bias, scale=scale)

        def mix_parts(t):
            nc.vector.scalar_tensor_tensor(near[t][:], gate[t][:], 1.0, h_banks[t][:], ALU.subtract, ALU.mult)
            nc.vector.tensor_tensor(far[t][:], wide[t][:].indirect(n5_t[:]), gate[t][:], ALU.mult)

        def mix_and_store(t):
            nc.vector.tensor_tensor(res[t][:], far[t][:], near[t][:], ALU.subtract)
            nc.sync.dma_start(out=out[t * P:(t + 1) * P, :], in_=res[t][:])

        nc.vector.tensor_copy(wide[0][:, :S], h_banks[0][:])
        nc.vector.tensor_copy(wide[1][:, :S], h_banks[1][:])
        gate_of(0)
        gate_of(1)
        nc.scalar.copy(wide[2][:, :S], h_banks[2][:])
        nc.scalar.copy(wide[3][:, :S], h_banks[3][:])
        gate_of(2)
        last = PACK - 1
        nc.scalar.activation(far[last][:], wide[last][:].indirect(n5_t[:]), ACT.Copy)
        gate_of(last)
        step = [sb([P, S], F32, "step_%d" % t) for t in range(2)]
        nc.vector.tensor_copy(far[0][:], wide[0][:].indirect(n5_t[:]))
        nc.vector.tensor_tensor(near[0][:], far[0][:], h_banks[0][:], ALU.subtract)
        mix_parts(1)
        nc.vector.tensor_tensor(step[0][:], near[0][:], gate[0][:], ALU.mult)
        nc.vector.tensor_tensor(res[0][:], step[0][:], h_banks[0][:], ALU.add)
        nc.sync.dma_start(out=out[:P, :], in_=res[0][:])
        mix_and_store(1)
        mix_parts(2)
        nc.vector.tensor_tensor(near[last][:], far[last][:], h_banks[last][:], ALU.subtract)
        mix_and_store(2)
        for lo, hi in halves:
            nc.vector.tensor_tensor(step[1][:, lo:hi], near[last][:, lo:hi], gate[last][:, lo:hi], ALU.mult)
        for lo, hi in halves:
            nc.vector.tensor_tensor(res[last][:, lo:hi], step[1][:, lo:hi], h_banks[last][:, lo:hi], ALU.add)
            nc.sync.dma_start(out=out[last * P:, lo:hi], in_=res[last][:, lo:hi])
